import numpy as np, ml_dtypes
CORES = [8,80,112,136,208,240,264,336,368,392,464,496]
N = 12
F = 512
GROUPS = [[0,1,2,3,4,5],[6,7,8,9,10,11]]
def setup_inputs(rng):
    return {"x": rng.standard_normal((N, 128, F), dtype=np.float32).astype(ml_dtypes.bfloat16), "w": (rng.standard_normal((N, 128, 128), dtype=np.float32) / 11).astype(ml_dtypes.bfloat16)}
def setup_inputs_big(rng):
    d = setup_inputs(rng)
    for k in ("x", "w"): d[k] = (d[k].astype(np.float32) * 1024.0).astype(d[k].dtype)
    return d
def setup_inputs_small(rng):
    d = setup_inputs(rng)
    for k in ("x", "w"): d[k] = (d[k].astype(np.float32) * (1 / 1024.0)).astype(d[k].dtype)
    return d
def setup_inputs_apart(rng):
    d = setup_inputs(rng)
    f = (10.0 ** rng.permutation(np.linspace(-1.5, 1.5, N))).astype(np.float32).reshape(N, 1, 1)
    for k in ("x", "w"): d[k] = (d[k].astype(np.float32) * f).astype(d[k].dtype)
    return d
def reference(x, w):
    X, W = x.astype(np.float64), w.astype(np.float64)
    s = sum(W[g[0]].T @ np.maximum(sum(X[j] for j in g), 0.0) for g in GROUPS).astype(ml_dtypes.bfloat16)
    return {"y": np.broadcast_to(s, (N,) + s.shape)}

@@ -1,0 +1,212 @@
+from concourse.bass import DstId, RemoteDMATransfer
+from concourse.mybir import AluOpType
+
+NCORES = 512
+F = 512
+S = 4
+NW = F // S
+
+SCRATCH = {
+    "xs": ("dram", [S, 128, NW], "bfloat16"),
+    "fin": ("dram", [4, 128, NW], "bfloat16"),
+    "wd": ("dram", [128, 128], "bfloat16"),
+    "pin": ("sbuf", [128, 4 * NW], "bfloat16"),
+    "wsb": ("sbuf", [128, 2 * 128], "bfloat16"),
+    "zero": ("sbuf", [128, NW], "float32"),
+    "tt": ("sbuf", [128, 2 * NW], "bfloat16"),
+    "yo": ("sbuf", [128, NW], "bfloat16"),
+    "yb": ("sbuf", [128, F], "bfloat16"),
+    "ps0": ("psum", [128, 512], "float32"),
+    "ps1": ("psum", [128, 512], "float32"),
+    "acc": ("psum", [128, 512], "float32"),
+}
+SEMAPHORES = ["ld", "wl", "fa", "pa0", "pa1", "wr", "wa", "z", "v", "t0", "t1", "mm", "yc", "ya", "st", "snt"]
+
+_CACHE = {}
+
+
+def _engines(mask):
+    return [e for e in range(16) if (mask >> e) & 1]
+
+
+def _bits(engs):
+    return sum(1 << e for e in engs)
+
+
+def _plan(T, topo):
+    if "p" in _CACHE:
+        return _CACHE["p"]
+    cores = list(T.cores)
+    on = {}
+    for c in range(NCORES):
+        on.setdefault((topo.host(c), topo.chip(c)), []).append(c)
+    hosts = sorted({h for h, _ in on})
+    chips = sorted({k for _, k in on})
+
+    def reach(a, b):
+        return a == b or topo.may_write(on[(a, chips[0])][0], on[(b, chips[0])][0])
+
+    def mate(k):
+        return [m for m in chips if topo.mates(on[(hosts[0], k)][0], on[(hosts[0], m)][0])][0]
+
+    def owners(h, k):
+        other = on[(h, mate(k))][0]
+        return [c for c in on[(h, k)] if topo.may_write(c, other)]
+
+    mem = [[cores[r] for r in grp] for grp in T.tables["GROUPS"]]
+    wown = [m[0] for m in mem]
+    racks = [topo.rack(topo.host(m[0])) for m in mem]
+    ng = len(mem)
+    hubh = [[h for h in hosts if topo.rack(h) == racks[g] and all(reach(topo.host(w), h) for w in wown)][0]
+            for g in range(ng)]
+    foldh = [[h for h in hosts if topo.rack(h) == racks[g] and all(reach(h, x) for x in hubh)][0] for g in range(ng)]
+    classes = []
+    for m in mem:
+        cl = []
+        for c in m:
+            for lst in cl:
+                if topo.same_plane(c, lst[0]):
+                    lst.append(c)
+                    break
+            else:
+                cl.append([c])
+        cl.sort(key=lambda lst: -len(lst))
+        classes.append(cl)
+    rankchips = {topo.chip(c) for c in cores}
+    lead = classes[0][0][0]
+
+    def like(k):
+        c = on[(topo.host(lead), k)][0]
+        return topo.chip(lead) == k or topo.same_plane(c, lead)
+
+    cand = [k for k in chips if like(k) and mate(k) not in rankchips]
+    cand.sort(key=lambda k: (k not in rankchips, k))
+    E = cand[:S]
+    p = {
+        "mem": mem, "wown": wown, "classes": classes,
+        "hub": [[owners(hubh[g], E[s])[s] for s in range(S)] for g in range(ng)],
+        "fold": [[[owners(foldh[g], E[s])[s] for s in range(S)],
+                  [owners(foldh[g], mate(E[s]))[s] for s in range(S)]] for g in range(ng)],
+        "relay": [[owners(topo.host(w), topo.chip(w))[s] for s in range(S)] for w in wown],
+    }
+    _CACHE["p"] = p
+    return p
+
+
+def _dst(topo, d, src):
+    rid, pid = topo.addr(d, src)
+    return DstId(rid=rid, pnc=pid)
+
+
+def _common(topo, src, dsts):
+    m = topo.mask(src, dsts[0])
+    for d in dsts[1:]:
+        m &= topo.mask(src, d)
+    return _engines(m)
+
+
+def rank_program(g, core, T, topo):
+    p = _plan(T, topo)
+    sem = T.sem
+    ng = len(p["mem"])
+
+    if T.rank_of(core) is not None:
+        grp = [i for i in range(ng) if core in p["mem"][i]][0]
+        cls = [i for i in range(2) if core in p["classes"][grp][i]][0]
+        slot = p["classes"][grp][cls].index(core)
+        folds = p["fold"][grp][cls]
+        owner = core == p["wown"][grp]
+        if owner:
+            g.sync.dma_start(T.wd[:], T.w[:]).then_inc(sem.wl, 16)
+        queues = [g.scalar, g.sync]
+        for s in range(S):
+            queues[s % 2].dma_start(T.xs[s], T.x[:, s * NW:(s + 1) * NW]).then_inc(sem.ld, 16)
+        eng = _common(topo, core, folds)
+        sent = 0
+        if owner:
+            relays = p["relay"][grp]
+            spare = [e for e in _common(topo, core, relays) if e not in eng]
+            g.wait_ge(sem.wl, 16)
+            g.remote_dma_fused([RemoteDMATransfer(
+                dst_ids=[_dst(topo, r, core) for r in relays], dma_engine_mask=_bits(spare), remote_sem=sem.wr,
+                srcs=[T.wd[:]], dsts=[T.wd[:] for _ in relays], alu_op=0)], local_sem=sem.snt)
+            sent += len(spare)
+        per = len(eng) // S
+        g.wait_ge(sem.ld, 16 * S)
+        g.remote_dma_fused([RemoteDMATransfer(
+            dst_ids=[_dst(topo, folds[s], core)], dma_engine_mask=_bits(eng[s * per:(s + 1) * per]), remote_sem=sem.fa,
+            srcs=[T.xs[s]], dsts=[T.fin[slot]], alu_op=0) for s in range(S)], local_sem=sem.snt)
+        sent += per * S
+        hubs = p["hub"][grp]
+        arrive = sum(len(_common(topo, h, p["mem"][grp])) for h in hubs)
+        g.sync.wait_ge(sem.ya, arrive)
+        g.sync.dma_start(T.y[:], T.yb[:]).then_inc(sem.st, 16)
+        g.sync.wait_ge(sem.st, 16)
+        g.wait_ge(sem.snt, sent)
+        return
+
+    for grp in range(ng):
+        for cls in range(2):
+            if core in p["fold"][grp][cls]:
+                s = p["fold"][grp][cls].index(core)
+                members = p["classes"][grp][cls]
+                per = len(_common(topo, members[0], p["fold"][grp][cls])) // S
+                hubs = [p["hub"][i][s] for i in range(ng)]
+                eng = _common(topo, core, hubs)
+                k = 2 * grp + cls
+                g.wait_ge(sem.fa, per * len(members))
+                g.remote_dma_fused([RemoteDMATransfer(
+                    dst_ids=[_dst(topo, h, core) for h in hubs], dma_engine_mask=_bits(eng),
+                    remote_sem=sem["pa%d" % grp], srcs=[T.fin[i] for i in range(len(members))],
+                    dsts=[T.pin[:, k * NW:(k + 1) * NW] for _ in hubs], alu_op=1)], local_sem=sem.snt)
+                g.wait_ge(sem.snt, len(eng))
+                return
+        if core in p["relay"][grp]:
+            s = p["relay"][grp].index(core)
+            w = p["wown"][grp]
+            got = len([e for e in _common(topo, w, p["relay"][grp])
+                       if e not in _common(topo, w, p["fold"][grp][[i for i in range(2) if w in p["classes"][grp][i]][0]])])
+            hubs = [p["hub"][i][s] for i in range(ng)]
+            eng = _common(topo, core, hubs)
+            g.wait_ge(sem.wr, got)
+            g.remote_dma_fused([RemoteDMATransfer(
+                dst_ids=[_dst(topo, h, core) for h in hubs], dma_engine_mask=_bits(eng), remote_sem=sem.wa,
+                srcs=[T.wd[:]], dsts=[T.wsb[:, grp * 128:(grp + 1) * 128] for _ in hubs], alu_op=0)],
+                local_sem=sem.snt)
+            g.wait_ge(sem.snt, len(eng))
+            return
+
+    for own in range(ng):
+        if core in p["hub"][own]:
+            s = p["hub"][own].index(core)
+            v, pe = g.vector, g.tensor
+            order = [own] + [i for i in range(ng) if i != own]
+            psum = [T.ps0, T.ps1]
+            v.memset(T.zero[:], 0.0).then_inc(sem.z, 1)
+            v.wait_ge(sem.z, 1)
+            wgot = 0
+            for i in range(ng):
+                wgot += len(_common(topo, p["relay"][i][s], [p["hub"][j][s] for j in range(ng)]))
+            pe.wait_ge(sem.wa, wgot)
+            for n, i in enumerate(order):
+                got = sum(len(_common(topo, p["fold"][i][c][s], [p["hub"][j][s] for j in range(ng)])) for c in range(2))
+                v.wait_ge(sem["pa%d" % i], got)
+                v.tensor_tensor(psum[n][:, 0:NW], T.pin[:, 2 * i * NW:(2 * i + 1) * NW],
+                                T.pin[:, (2 * i + 1) * NW:(2 * i + 2) * NW], AluOpType.add).then_inc(sem.v, 1)
+                v.wait_ge(sem.v, n + 1)
+                v.tensor_tensor(T.tt[:, i * NW:(i + 1) * NW], psum[n][:, 0:NW], T.zero[:],
+                                AluOpType.max).then_inc(sem["t%d" % i], 1)
+                pe.wait_ge(sem["t%d" % i], 1)
+                mm = pe.matmul(T.acc[:, 0:NW], T.wsb[:, i * 128:(i + 1) * 128], T.tt[:, i * NW:(i + 1) * NW],
+                               n == 0, n == ng - 1)
+            mm.then_inc(sem.mm, 1)
+            v.wait_ge(sem.mm, 1)
+            v.tensor_copy(T.yo[:], T.acc[:, 0:NW]).then_inc(sem.yc, 1)
+            ranks = p["mem"][own]
+            eng = _common(topo, core, ranks)
+            g.wait_ge(sem.yc, 1)
+            g.remote_dma_fused([RemoteDMATransfer(
+                dst_ids=[_dst(topo, r, core) for r in ranks], dma_engine_mask=_bits(eng), remote_sem=sem.ya,
+                srcs=[T.yo[:]], dsts=[T.yb[:, s * NW:(s + 1) * NW] for _ in ranks], alu_op=0)], local_sem=sem.snt)
+            g.wait_ge(sem.snt, len(eng))
+            return

@@ -5,6 +5,7 @@ NCORES = 512
 F = 512
 S = 4
 NW = F // S
+NQ = 2
 
 SCRATCH = {
     "xs": ("dram", [S, 128, NW], "bfloat16"),
@@ -20,7 +21,7 @@ SCRATCH = {
     "ps1": ("psum", [128, 512], "float32"),
     "acc": ("psum", [128, 512], "float32"),
 }
-SEMAPHORES = ["ld", "wl", "fa", "pa0", "pa1", "wr", "wa", "z", "v", "t0", "t1", "mm", "yc", "ya", "st", "snt"]
+SEMAPHORES = ["ld", "wl", "fa", "pa0", "pa1", "wr", "wa0", "wa1", "z", "v", "t0", "t1", "mm", "yc", "ya", "st", "snt"]
 
 _CACHE = {}
 
@@ -31,6 +32,18 @@ def _engines(mask):
 
 def _bits(engs):
     return sum(1 << e for e in engs)
+
+
+def _dst(topo, d, src):
+    rid, pid = topo.addr(d, src)
+    return DstId(rid=rid, pnc=pid)
+
+
+def _common(topo, src, dsts):
+    m = topo.mask(src, dsts[0])
+    for d in dsts[1:]:
+        m &= topo.mask(src, d)
+    return _engines(m)
 
 
 def _plan(T, topo):
@@ -53,13 +66,15 @@ def _plan(T, topo):
         other = on[(h, mate(k))][0]
         return [c for c in on[(h, k)] if topo.may_write(c, other)]
 
+    def tau(s):
+        return (s + S // 2) % S
+
     mem = [[cores[r] for r in grp] for grp in T.tables["GROUPS"]]
     wown = [m[0] for m in mem]
     racks = [topo.rack(topo.host(m[0])) for m in mem]
     ng = len(mem)
-    hubh = [[h for h in hosts if topo.rack(h) == racks[g] and all(reach(topo.host(w), h) for w in wown)][0]
-            for g in range(ng)]
-    foldh = [[h for h in hosts if topo.rack(h) == racks[g] and all(reach(h, x) for x in hubh)][0] for g in range(ng)]
+    wh = [[a, b] for a in hosts for b in hosts
+          if topo.rack(a) == racks[0] and topo.rack(b) == racks[1] and reach(a, b) and reach(b, a)][0]
     classes = []
     for m in mem:
         cl = []
@@ -82,27 +97,69 @@ def _plan(T, topo):
     cand = [k for k in chips if like(k) and mate(k) not in rankchips]
     cand.sort(key=lambda k: (k not in rankchips, k))
     E = cand[:S]
-    p = {
-        "mem": mem, "wown": wown, "classes": classes,
-        "hub": [[owners(hubh[g], E[s])[s] for s in range(S)] for g in range(ng)],
-        "fold": [[[owners(foldh[g], E[s])[s] for s in range(S)],
-                  [owners(foldh[g], mate(E[s]))[s] for s in range(S)]] for g in range(ng)],
-        "relay": [[owners(topo.host(w), topo.chip(w))[s] for s in range(S)] for w in wown],
-    }
+    wchip = [[E[s] if g == 0 else E[tau(s)] for s in range(S)] for g in range(ng)]
+    work = [[owners(wh[g], wchip[g][s])[s] for s in range(S)] for g in range(ng)]
+    odd = [[owners(wh[g], mate(wchip[g][s]))[s] for s in range(S)] for g in range(ng)]
+    hub = [[work[g][tau(s)] for s in range(S)] for g in range(ng)]
+
+    near, far, fwd, wgot = [], [], {}, {}
+    for g, w in enumerate(wown):
+        hw = topo.host(w)
+        cls = [i for i in range(2) if w in classes[g][i]][0]
+        xeng = _common(topo, w, [work, odd][cls][g])
+        ok = [i for i in range(ng) if reach(hw, wh[i])]
+        relays = [owners(hw, topo.chip(w))[s] for s in range(S)]
+        spare = [e for e in _common(topo, w, relays) if e not in xeng]
+        near.append((relays, spare))
+        for s, r in enumerate(relays):
+            fwd[r] = (g, len(spare), [hub[i][s] for i in ok])
+        qs = []
+        for i in range(ng):
+            if i in ok:
+                continue
+            hq = [h for h in hosts if topo.rack(h) == topo.rack(wh[i]) and reach(hw, h) and reach(h, wh[i])][0]
+            own = owners(hq, topo.chip(w))
+            step = len(own) // NQ
+            for j in range(NQ):
+                qs.append((own[j * step], [hub[i][s] for s in range(j * S // NQ, (j + 1) * S // NQ)]))
+        qeng = _common(topo, w, [q for q, _ in qs]) if qs else []
+        far.append(([q for q, _ in qs], qeng))
+        for q, dsts in qs:
+            fwd[q] = (g, len(qeng), dsts)
+    for c, (g, _, dsts) in fwd.items():
+        for d in dsts:
+            wgot[(d, g)] = len(_common(topo, c, dsts))
+    p = {"mem": mem, "wown": wown, "classes": classes, "hub": hub, "fold": [[work[g], odd[g]] for g in range(ng)],
+         "near": near, "far": far, "fwd": fwd, "wgot": wgot}
     _CACHE["p"] = p
     return p
 
 
-def _dst(topo, d, src):
-    rid, pid = topo.addr(d, src)
-    return DstId(rid=rid, pnc=pid)
+def _fold(g, core, T, topo, p, grp, cls):
+    sem = T.sem
+    ng = len(p["mem"])
+    s = p["fold"][grp][cls].index(core)
+    members = p["classes"][grp][cls]
+    per = len(_common(topo, members[0], p["fold"][grp][cls])) // S
+    hubs = [p["hub"][i][s] for i in range(ng)]
+    eng = _common(topo, core, hubs)
+    k = 2 * grp + cls
+    g.wait_ge(sem.fa, per * len(members))
+    g.remote_dma_fused([RemoteDMATransfer(
+        dst_ids=[_dst(topo, h, core) for h in hubs], dma_engine_mask=_bits(eng),
+        remote_sem=sem["pa%d" % grp], srcs=[T.fin[i] for i in range(len(members))],
+        dsts=[T.pin[:, k * NW:(k + 1) * NW] for _ in hubs], alu_op=1)], local_sem=sem.snt)
+    return len(eng)
 
 
-def _common(topo, src, dsts):
-    m = topo.mask(src, dsts[0])
-    for d in dsts[1:]:
-        m &= topo.mask(src, d)
-    return _engines(m)
+def _send_w(g, core, T, topo, route):
+    fw, fe = route
+    if not fw:
+        return 0
+    g.remote_dma_fused([RemoteDMATransfer(
+        dst_ids=[_dst(topo, r, core) for r in fw], dma_engine_mask=_bits(fe), remote_sem=T.sem.wr,
+        srcs=[T.wd[:]], dsts=[T.wd[:] for _ in fw], alu_op=0)], local_sem=T.sem.snt)
+    return len(fe)
 
 
 def rank_program(g, core, T, topo):
@@ -124,70 +181,46 @@ def rank_program(g, core, T, topo):
         eng = _common(topo, core, folds)
         sent = 0
         if owner:
-            relays = p["relay"][grp]
-            spare = [e for e in _common(topo, core, relays) if e not in eng]
             g.wait_ge(sem.wl, 16)
-            g.remote_dma_fused([RemoteDMATransfer(
-                dst_ids=[_dst(topo, r, core) for r in relays], dma_engine_mask=_bits(spare), remote_sem=sem.wr,
-                srcs=[T.wd[:]], dsts=[T.wd[:] for _ in relays], alu_op=0)], local_sem=sem.snt)
-            sent += len(spare)
+            sent += _send_w(g, core, T, topo, p["near"][grp])
         per = len(eng) // S
         g.wait_ge(sem.ld, 16 * S)
         g.remote_dma_fused([RemoteDMATransfer(
             dst_ids=[_dst(topo, folds[s], core)], dma_engine_mask=_bits(eng[s * per:(s + 1) * per]), remote_sem=sem.fa,
             srcs=[T.xs[s]], dsts=[T.fin[slot]], alu_op=0) for s in range(S)], local_sem=sem.snt)
         sent += per * S
-        hubs = p["hub"][grp]
-        arrive = sum(len(_common(topo, h, p["mem"][grp])) for h in hubs)
+        if owner:
+            sent += _send_w(g, core, T, topo, p["far"][grp])
+        arrive = sum(len(_common(topo, h, p["mem"][grp])) for h in p["hub"][grp])
         g.sync.wait_ge(sem.ya, arrive)
         g.sync.dma_start(T.y[:], T.yb[:]).then_inc(sem.st, 16)
         g.sync.wait_ge(sem.st, 16)
         g.wait_ge(sem.snt, sent)
         return
 
-    for grp in range(ng):
-        for cls in range(2):
-            if core in p["fold"][grp][cls]:
-                s = p["fold"][grp][cls].index(core)
-                members = p["classes"][grp][cls]
-                per = len(_common(topo, members[0], p["fold"][grp][cls])) // S
-                hubs = [p["hub"][i][s] for i in range(ng)]
-                eng = _common(topo, core, hubs)
-                k = 2 * grp + cls
-                g.wait_ge(sem.fa, per * len(members))
-                g.remote_dma_fused([RemoteDMATransfer(
-                    dst_ids=[_dst(topo, h, core) for h in hubs], dma_engine_mask=_bits(eng),
-                    remote_sem=sem["pa%d" % grp], srcs=[T.fin[i] for i in range(len(members))],
-                    dsts=[T.pin[:, k * NW:(k + 1) * NW] for _ in hubs], alu_op=1)], local_sem=sem.snt)
-                g.wait_ge(sem.snt, len(eng))
-                return
-        if core in p["relay"][grp]:
-            s = p["relay"][grp].index(core)
-            w = p["wown"][grp]
-            got = len([e for e in _common(topo, w, p["relay"][grp])
-                       if e not in _common(topo, w, p["fold"][grp][[i for i in range(2) if w in p["classes"][grp][i]][0]])])
-            hubs = [p["hub"][i][s] for i in range(ng)]
-            eng = _common(topo, core, hubs)
-            g.wait_ge(sem.wr, got)
-            g.remote_dma_fused([RemoteDMATransfer(
-                dst_ids=[_dst(topo, h, core) for h in hubs], dma_engine_mask=_bits(eng), remote_sem=sem.wa,
-                srcs=[T.wd[:]], dsts=[T.wsb[:, grp * 128:(grp + 1) * 128] for _ in hubs], alu_op=0)],
-                local_sem=sem.snt)
-            g.wait_ge(sem.snt, len(eng))
-            return
+    if core in p["fwd"]:
+        grp, got, hubs = p["fwd"][core]
+        eng = _common(topo, core, hubs)
+        g.wait_ge(sem.wr, got)
+        g.remote_dma_fused([RemoteDMATransfer(
+            dst_ids=[_dst(topo, h, core) for h in hubs], dma_engine_mask=_bits(eng), remote_sem=sem["wa%d" % grp],
+            srcs=[T.wd[:]], dsts=[T.wsb[:, grp * 128:(grp + 1) * 128] for _ in hubs], alu_op=0)],
+            local_sem=sem.snt)
+        g.wait_ge(sem.snt, len(eng))
+        return
 
     for own in range(ng):
-        if core in p["hub"][own]:
+        if core in p["fold"][own][1]:
+            g.wait_ge(sem.snt, _fold(g, core, T, topo, p, own, 1))
+            return
+        if core in p["fold"][own][0]:
+            sent = _fold(g, core, T, topo, p, own, 0)
             s = p["hub"][own].index(core)
             v, pe = g.vector, g.tensor
             order = [own] + [i for i in range(ng) if i != own]
             psum = [T.ps0, T.ps1]
             v.memset(T.zero[:], 0.0).then_inc(sem.z, 1)
             v.wait_ge(sem.z, 1)
-            wgot = 0
-            for i in range(ng):
-                wgot += len(_common(topo, p["relay"][i][s], [p["hub"][j][s] for j in range(ng)]))
-            pe.wait_ge(sem.wa, wgot)
             for n, i in enumerate(order):
                 got = sum(len(_common(topo, p["fold"][i][c][s], [p["hub"][j][s] for j in range(ng)])) for c in range(2))
                 v.wait_ge(sem["pa%d" % i], got)
@@ -196,6 +229,7 @@ def rank_program(g, core, T, topo):
                 v.wait_ge(sem.v, n + 1)
                 v.tensor_tensor(T.tt[:, i * NW:(i + 1) * NW], psum[n][:, 0:NW], T.zero[:],
                                 AluOpType.max).then_inc(sem["t%d" % i], 1)
+                pe.wait_ge(sem["wa%d" % i], p["wgot"][(core, i)])
                 pe.wait_ge(sem["t%d" % i], 1)
                 mm = pe.matmul(T.acc[:, 0:NW], T.wsb[:, i * 128:(i + 1) * 128], T.tt[:, i * NW:(i + 1) * NW],
                                n == 0, n == ng - 1)
@@ -208,5 +242,5 @@ def rank_program(g, core, T, topo):
             g.remote_dma_fused([RemoteDMATransfer(
                 dst_ids=[_dst(topo, r, core) for r in ranks], dma_engine_mask=_bits(eng), remote_sem=sem.ya,
                 srcs=[T.yo[:]], dsts=[T.yb[:, s * NW:(s + 1) * NW] for _ in ranks], alu_op=0)], local_sem=sem.snt)
-            g.wait_ge(sem.snt, len(eng))
+            g.wait_ge(sem.snt, sent + len(eng))
             return

from concourse.bass import DstId, RemoteDMATransfer
from concourse.mybir import AluOpType

NCORES = 512
F = 512
S = 4
NW = F // S
NQ = 2

SCRATCH = {
    "xs": ("dram", [S, 128, NW], "bfloat16"),
    "fin": ("dram", [4, 128, NW], "bfloat16"),
    "wd": ("dram", [128, 128], "bfloat16"),
    "pin": ("sbuf", [128, 4 * NW], "bfloat16"),
    "wsb": ("sbuf", [128, 2 * 128], "bfloat16"),
    "zero": ("sbuf", [128, NW], "float32"),
    "tt": ("sbuf", [128, 2 * NW], "bfloat16"),
    "yo": ("sbuf", [128, NW], "bfloat16"),
    "yb": ("sbuf", [128, F], "bfloat16"),
    "ps0": ("psum", [128, 512], "float32"),
    "ps1": ("psum", [128, 512], "float32"),
    "acc": ("psum", [128, 512], "float32"),
}
SEMAPHORES = ["ld", "wl", "fa", "pa0", "pa1", "wr", "wa0", "wa1", "z", "v", "t0", "t1", "mm", "yc", "ya", "st", "snt"]

_CACHE = {}


def _engines(mask):
    return [e for e in range(16) if (mask >> e) & 1]


def _bits(engs):
    return sum(1 << e for e in engs)


def _dst(topo, d, src):
    rid, pid = topo.addr(d, src)
    return DstId(rid=rid, pnc=pid)


def _common(topo, src, dsts):
    m = topo.mask(src, dsts[0])
    for d in dsts[1:]:
        m &= topo.mask(src, d)
    return _engines(m)


def _plan(T, topo):
    if "p" in _CACHE:
        return _CACHE["p"]
    cores = list(T.cores)
    on = {}
    for c in range(NCORES):
        on.setdefault((topo.host(c), topo.chip(c)), []).append(c)
    hosts = sorted({h for h, _ in on})
    chips = sorted({k for _, k in on})

    def reach(a, b):
        return a == b or topo.may_write(on[(a, chips[0])][0], on[(b, chips[0])][0])

    def mate(k):
        return [m for m in chips if topo.mates(on[(hosts[0], k)][0], on[(hosts[0], m)][0])][0]

    def owners(h, k):
        other = on[(h, mate(k))][0]
        return [c for c in on[(h, k)] if topo.may_write(c, other)]

    def tau(s):
        return (s + S // 2) % S

    mem = [[cores[r] for r in grp] for grp in T.tables["GROUPS"]]
    wown = [m[0] for m in mem]
    racks = [topo.rack(topo.host(m[0])) for m in mem]
    ng = len(mem)
    wh = [[a, b] for a in hosts for b in hosts
          if topo.rack(a) == racks[0] and topo.rack(b) == racks[1] and reach(a, b) and reach(b, a)][0]
    classes = []
    for m in mem:
        cl = []
        for c in m:
            for lst in cl:
                if topo.same_plane(c, lst[0]):
                    lst.append(c)
                    break
            else:
                cl.append([c])
        cl.sort(key=lambda lst: -len(lst))
        classes.append(cl)
    rankchips = {topo.chip(c) for c in cores}
    lead = classes[0][0][0]

    def like(k):
        c = on[(topo.host(lead), k)][0]
        return topo.chip(lead) == k or topo.same_plane(c, lead)

    cand = [k for k in chips if like(k) and mate(k) not in rankchips]
    cand.sort(key=lambda k: (k not in rankchips, k))
    E = cand[:S]
    wchip = [[E[s] if g == 0 else E[tau(s)] for s in range(S)] for g in range(ng)]
    work = [[owners(wh[g], wchip[g][s])[s] for s in range(S)] for g in range(ng)]
    odd = [[owners(wh[g], mate(wchip[g][s]))[s] for s in range(S)] for g in range(ng)]
    hub = [[work[g][tau(s)] for s in range(S)] for g in range(ng)]

    near, far, fwd, wgot = [], [], {}, {}
    for g, w in enumerate(wown):
        hw = topo.host(w)
        cls = [i for i in range(2) if w in classes[g][i]][0]
        xeng = _common(topo, w, [work, odd][cls][g])
        ok = [i for i in range(ng) if reach(hw, wh[i])]
        relays = [owners(hw, topo.chip(w))[s] for s in range(S)]
        spare = [e for e in _common(topo, w, relays) if e not in xeng]
        near.append((relays, spare))
        for s, r in enumerate(relays):
            fwd[r] = (g, len(spare), [hub[i][s] for i in ok])
        qs = []
        for i in range(ng):
            if i in ok:
                continue
            hq = [h for h in hosts if topo.rack(h) == topo.rack(wh[i]) and reach(hw, h) and reach(h, wh[i])][0]
            own = owners(hq, topo.chip(w))
            step = len(own) // NQ
            for j in range(NQ):
                qs.append((own[j * step], [hub[i][s] for s in range(j * S // NQ, (j + 1) * S // NQ)]))
        qeng = _common(topo, w, [q for q, _ in qs]) if qs else []
        far.append(([q for q, _ in qs], qeng))
        for q, dsts in qs:
            fwd[q] = (g, len(qeng), dsts)
    for c, (g, _, dsts) in fwd.items():
        for d in dsts:
            wgot[(d, g)] = len(_common(topo, c, dsts))
    p = {"mem": mem, "wown": wown, "classes": classes, "hub": hub, "fold": [[work[g], odd[g]] for g in range(ng)],
         "near": near, "far": far, "fwd": fwd, "wgot": wgot}
    _CACHE["p"] = p
    return p


def _fold(g, core, T, topo, p, grp, cls):
    sem = T.sem
    ng = len(p["mem"])
    s = p["fold"][grp][cls].index(core)
    members = p["classes"][grp][cls]
    per = len(_common(topo, members[0], p["fold"][grp][cls])) // S
    hubs = [p["hub"][i][s] for i in range(ng)]
    eng = _common(topo, core, hubs)
    k = 2 * grp + cls
    g.wait_ge(sem.fa, per * len(members))
    g.remote_dma_fused([RemoteDMATransfer(
        dst_ids=[_dst(topo, h, core) for h in hubs], dma_engine_mask=_bits(eng),
        remote_sem=sem["pa%d" % grp], srcs=[T.fin[i] for i in range(len(members))],
        dsts=[T.pin[:, k * NW:(k + 1) * NW] for _ in hubs], alu_op=1)], local_sem=sem.snt)
    return len(eng)


def _send_w(g, core, T, topo, route):
    fw, fe = route
    if not fw:
        return 0
    g.remote_dma_fused([RemoteDMATransfer(
        dst_ids=[_dst(topo, r, core) for r in fw], dma_engine_mask=_bits(fe), remote_sem=T.sem.wr,
        srcs=[T.wd[:]], dsts=[T.wd[:] for _ in fw], alu_op=0)], local_sem=T.sem.snt)
    return len(fe)


def rank_program(g, core, T, topo):
    p = _plan(T, topo)
    sem = T.sem
    ng = len(p["mem"])

    if T.rank_of(core) is not None:
        grp = [i for i in range(ng) if core in p["mem"][i]][0]
        cls = [i for i in range(2) if core in p["classes"][grp][i]][0]
        slot = p["classes"][grp][cls].index(core)
        folds = p["fold"][grp][cls]
        owner = core == p["wown"][grp]
        if owner:
            g.sync.dma_start(T.wd[:], T.w[:]).then_inc(sem.wl, 16)
        queues = [g.scalar, g.sync]
        for s in range(S):
            queues[s % 2].dma_start(T.xs[s], T.x[:, s * NW:(s + 1) * NW]).then_inc(sem.ld, 16)
        eng = _common(topo, core, folds)
        sent = 0
        if owner:
            g.wait_ge(sem.wl, 16)
            sent += _send_w(g, core, T, topo, p["near"][grp])
        per = len(eng) // S
        g.wait_ge(sem.ld, 16 * S)
        g.remote_dma_fused([RemoteDMATransfer(
            dst_ids=[_dst(topo, folds[s], core)], dma_engine_mask=_bits(eng[s * per:(s + 1) * per]), remote_sem=sem.fa,
            srcs=[T.xs[s]], dsts=[T.fin[slot]], alu_op=0) for s in range(S)], local_sem=sem.snt)
        sent += per * S
        if owner:
            sent += _send_w(g, core, T, topo, p["far"][grp])
        arrive = sum(len(_common(topo, h, p["mem"][grp])) for h in p["hub"][grp])
        g.sync.wait_ge(sem.ya, arrive)
        g.sync.dma_start(T.y[:], T.yb[:]).then_inc(sem.st, 16)
        g.sync.wait_ge(sem.st, 16)
        g.wait_ge(sem.snt, sent)
        return

    if core in p["fwd"]:
        grp, got, hubs = p["fwd"][core]
        eng = _common(topo, core, hubs)
        g.wait_ge(sem.wr, got)
        g.remote_dma_fused([RemoteDMATransfer(
            dst_ids=[_dst(topo, h, core) for h in hubs], dma_engine_mask=_bits(eng), remote_sem=sem["wa%d" % grp],
            srcs=[T.wd[:]], dsts=[T.wsb[:, grp * 128:(grp + 1) * 128] for _ in hubs], alu_op=0)],
            local_sem=sem.snt)
        g.wait_ge(sem.snt, len(eng))
        return

    for own in range(ng):
        if core in p["fold"][own][1]:
            g.wait_ge(sem.snt, _fold(g, core, T, topo, p, own, 1))
            return
        if core in p["fold"][own][0]:
            sent = _fold(g, core, T, topo, p, own, 0)
            s = p["hub"][own].index(core)
            v, pe = g.vector, g.tensor
            order = [own] + [i for i in range(ng) if i != own]
            psum = [T.ps0, T.ps1]
            v.memset(T.zero[:], 0.0).then_inc(sem.z, 1)
            v.wait_ge(sem.z, 1)
            for n, i in enumerate(order):
                got = sum(len(_common(topo, p["fold"][i][c][s], [p["hub"][j][s] for j in range(ng)])) for c in range(2))
                v.wait_ge(sem["pa%d" % i], got)
                v.tensor_tensor(psum[n][:, 0:NW], T.pin[:, 2 * i * NW:(2 * i + 1) * NW],
                                T.pin[:, (2 * i + 1) * NW:(2 * i + 2) * NW], AluOpType.add).then_inc(sem.v, 1)
                v.wait_ge(sem.v, n + 1)
                v.tensor_tensor(T.tt[:, i * NW:(i + 1) * NW], psum[n][:, 0:NW], T.zero[:],
                                AluOpType.max).then_inc(sem["t%d" % i], 1)
                pe.wait_ge(sem["wa%d" % i], p["wgot"][(core, i)])
                pe.wait_ge(sem["t%d" % i], 1)
                mm = pe.matmul(T.acc[:, 0:NW], T.wsb[:, i * 128:(i + 1) * 128], T.tt[:, i * NW:(i + 1) * NW],
                               n == 0, n == ng - 1)
            mm.then_inc(sem.mm, 1)
            v.wait_ge(sem.mm, 1)
            v.tensor_copy(T.yo[:], T.acc[:, 0:NW]).then_inc(sem.yc, 1)
            ranks = p["mem"][own]
            eng = _common(topo, core, ranks)
            g.wait_ge(sem.yc, 1)
            g.remote_dma_fused([RemoteDMATransfer(
                dst_ids=[_dst(topo, r, core) for r in ranks], dma_engine_mask=_bits(eng), remote_sem=sem.ya,
                srcs=[T.yo[:]], dsts=[T.yb[:, s * NW:(s + 1) * NW] for _ in ranks], alu_op=0)], local_sem=sem.snt)
            g.wait_ge(sem.snt, sent + len(eng))
            return
